import numpy as np, ml_dtypes
CORES = [76,84,92,100,108,116,124]
N = 7
F, TK = 128, 32
def setup_inputs(rng):
    return {"x": rng.standard_normal((N, 128, N * TK), dtype=np.float32).astype(ml_dtypes.bfloat16), "w": rng.standard_normal((N, 128, F), dtype=np.float32).astype(ml_dtypes.bfloat16)}
def setup_inputs_big(rng):
    d = setup_inputs(rng)
    for k in ("x", "w"): d[k] = (d[k].astype(np.float32) * 1024.0).astype(d[k].dtype)
    return d
def setup_inputs_small(rng):
    d = setup_inputs(rng)
    for k in ("x", "w"): d[k] = (d[k].astype(np.float32) * (1 / 1024.0)).astype(d[k].dtype)
    return d
def setup_inputs_apart(rng):
    d = setup_inputs(rng)
    f = (10.0 ** rng.permutation(np.linspace(-1.5, 1.5, N))).astype(np.float32).reshape(N, 1, 1)
    for k in ("x", "w"): d[k] = (d[k].astype(np.float32) * f).astype(d[k].dtype)
    return d
def reference(x, w):
    X, W = x.astype(np.float64), w.astype(np.float64)
    y = np.zeros((N, F, N * TK))
    for r in range(N):
        for j in range(N):
            y[r][:, TK * j:TK * j + TK] = W[r].T @ X[j][:, TK * r:TK * r + TK]
    return {"y": y.astype(ml_dtypes.bfloat16 if x.dtype != np.float64 else np.float64)}

@@ -1,0 +1,142 @@
+from concourse.bass import DstId, RemoteDMATransfer
+
+TK = 32
+NR = 7
+DIRECT = 2
+N1 = 4
+N2 = 8
+ND = 4
+
+SCRATCH = {
+    "xs": ("sbuf", [128, NR * TK], "bfloat16"),
+    "ws": ("sbuf", [128, 128], "bfloat16"),
+    "land": ("sbuf", [128, NR * TK], "bfloat16"),
+    "relay": ("sbuf", [128, TK], "bfloat16"),
+    "ys": ("sbuf", [128, NR * TK], "bfloat16"),
+    "acc": ("psum", [128, 512], "float32"),
+}
+SEMAPHORES = ["ldx", "ldw", "hop", "arrived", "sent", "mm", "cp", "st"]
+
+
+def _engines(mask):
+    return [e for e in range(mask.bit_length()) if (mask >> e) & 1]
+
+
+def _bits(engines):
+    m = 0
+    for e in engines:
+        m |= 1 << e
+    return m
+
+
+def _deal(src, dsts, per, topo):
+    common = topo.mask(src, dsts[0])
+    for d in dsts:
+        common &= topo.mask(src, d)
+    eng = _engines(common)
+    k = len(dsts)
+    eng = eng[len(eng) - k * per:]
+    return [_bits(eng[i::k]) for i in range(k)]
+
+
+def _plan(T, topo):
+    cores = list(T.cores)
+    n = len(cores)
+    everyone = range(topo.CHIPS * topo.CORES_PER_CHIP)
+    plan = []
+    for s, c in enumerate(cores):
+        peers = [(s + k) % n for k in range(1, n)]
+        far = [d for d in peers if not topo.may_write(c, cores[d])]
+        near = [d for d in peers if topo.may_write(c, cores[d])]
+        extra = max(0, len(near) - DIRECT)
+        free = [h for h in everyone if topo.chip(h) == topo.chip(c) and h not in cores]
+        free.sort(key=lambda h: (topo.die(h) != topo.die(c), h))
+        relay = []
+        for d in far + near[:extra]:
+            h = [h for h in free if topo.may_write(h, cores[d])]
+            if d not in far:
+                h = [q for q in h if not all(topo.may_write(q, x) for x in cores)] or h
+            relay.append((h[0], d))
+            free.remove(h[0])
+        a = [p for p in relay if topo.die(p[0]) == topo.die(c)]
+        b = [p for p in relay if topo.die(p[0]) != topo.die(c)]
+        mixed = []
+        while a or b:
+            if a:
+                mixed.append(a.pop(0))
+            if b:
+                mixed.append(b.pop(0))
+        plan.append({"relay": mixed, "direct": near[extra:]})
+    return plan
+
+
+def _dst(topo, c):
+    rid, pid, _ = topo.addr(c)
+    return DstId(rid=rid, pnc=pid)
+
+
+def _helper(g, core, T, topo, s, d):
+    to = T.cores[d]
+    eng = _engines(topo.mask(core, to))
+    step = len(eng) // N2
+    rid, pid, _ = topo.addr(to)
+    g.wait_ge(T.sem.hop, N1)
+    g.remote_dma(T.land[:, TK * s:TK * s + TK], T.relay[:], T.sem.arrived, T.sem.sent, pid, rid, _bits(eng[::step]))
+    g.wait_ge(T.sem.sent, N2)
+
+
+def rank_program(g, core, T, topo):
+    plan = _plan(T, topo)
+    rank = T.rank_of(core)
+    if rank is None:
+        for s, p in enumerate(plan):
+            for h, d in p["relay"]:
+                if h == core:
+                    _helper(g, core, T, topo, s, d)
+        return
+
+    mine = plan[rank]
+    cols = NR * TK
+    own = TK * rank
+
+    g.sync.dma_start(T.xs[:], T.x[:, :]).then_inc(T.sem.ldx, 16)
+    g.sync.dma_start(T.ws[:], T.w[:, :]).then_inc(T.sem.ldw, 16)
+
+    g.wait_ge(T.sem.ldx, 16)
+    helpers = [h for h, _ in mine["relay"]]
+    masks = _deal(core, helpers, N1, topo)
+    g.remote_dma_fused(
+        [RemoteDMATransfer(dst_ids=[_dst(topo, h)], dma_engine_mask=m, remote_sem=T.sem.hop,
+                           src=T.xs[:, TK * d:TK * d + TK], dst=T.relay[:])
+         for (h, d), m in zip(mine["relay"], masks)],
+        local_sem=T.sem.sent)
+    peers = [T.cores[d] for d in mine["direct"]]
+    masks = _deal(core, peers, ND, topo)
+    g.remote_dma_fused(
+        [RemoteDMATransfer(dst_ids=[_dst(topo, T.cores[d])], dma_engine_mask=m, remote_sem=T.sem.arrived,
+                           src=T.xs[:, TK * d:TK * d + TK], dst=T.land[:, own:own + TK])
+         for d, m in zip(mine["direct"], masks)],
+        local_sem=T.sem.sent)
+
+    expect = 0
+    for s, p in enumerate(plan):
+        expect += N2 * len([1 for _, d in p["relay"] if d == rank]) + ND * len([1 for d in p["direct"] if d == rank])
+
+    g.tensor.wait_ge(T.sem.ldw, 16)
+    g.tensor.wait_ge(T.sem.ldx, 16)
+    g.tensor.matmul(T.acc[:, own:own + TK], T.ws[:], T.xs[:, own:own + TK], start=True, stop=True).then_inc(T.sem.mm, 1)
+    g.tensor.wait_ge(T.sem.arrived, expect)
+    done = 1
+    for a, b in ((0, own), (own + TK, cols)):
+        if b > a:
+            g.tensor.matmul(T.acc[:, a:b], T.ws[:], T.land[:, a:b], start=True, stop=True).then_inc(T.sem.mm, 1)
+            done += 1
+
+    g.vector.wait_ge(T.sem.mm, done)
+    g.vector.tensor_copy(T.ys[:], T.acc[:, 0:cols]).then_inc(T.sem.cp, 1)
+
+    g.sync.wait_ge(T.sem.cp, 1)
+    g.sync.dma_start(T.y[:, :], T.ys[:]).then_inc(T.sem.st, 16)
+    g.sync.wait_ge(T.sem.st, 16)
+
+    g.wait_ge(T.sem.sent, N1 * len(mine["relay"]) + ND * len(mine["direct"]))

@@ -3,19 +3,24 @@ from concourse.bass import DstId, RemoteDMATransfer
 TK = 32
 NR = 7
 DIRECT = 2
-N1 = 4
+RELAYED = NR - 1 - DIRECT
+N1 = 2
 N2 = 8
 ND = 4
 
 SCRATCH = {
+    "xb": ("dram", [RELAYED, 128, TK], "bfloat16"),
     "xs": ("sbuf", [128, NR * TK], "bfloat16"),
     "ws": ("sbuf", [128, 128], "bfloat16"),
-    "land": ("sbuf", [128, NR * TK], "bfloat16"),
-    "relay": ("sbuf", [128, TK], "bfloat16"),
-    "ys": ("sbuf", [128, NR * TK], "bfloat16"),
-    "acc": ("psum", [128, 512], "float32"),
+    "land": ("sbuf", [128, (NR - 1) * TK], "bfloat16"),
+    "relay": ("dram", [128, TK], "bfloat16"),
+    "ys": ("sbuf", [128, NR, TK], "bfloat16"),
+    "acco": ("psum", [128, 512], "float32"),
+    "acce": ("psum", [128, 512], "float32"),
+    "acc1": ("psum", [128, 512], "float32"),
+    "acc2": ("psum", [128, 512], "float32"),
 }
-SEMAPHORES = ["ldx", "ldw", "hop", "arrived", "sent", "mm", "cp", "st"]
+SEMAPHORES = ["ldb", "ldx", "ldw", "hop", "arre", "arrl", "sent", "mmo", "mme", "mm1", "mm2", "cp", "st"]
 
 
 def _engines(mask):
@@ -29,13 +34,16 @@ def _bits(engines):
     return m
 
 
-def _deal(src, dsts, per, topo):
-    common = topo.mask(src, dsts[0])
+def _common(topo, src, dsts):
+    m = topo.mask(src, dsts[0])
     for d in dsts:
-        common &= topo.mask(src, d)
-    eng = _engines(common)
-    k = len(dsts)
-    eng = eng[len(eng) - k * per:]
+        m &= topo.mask(src, d)
+    return _engines(m)
+
+
+def _deal(eng, k, per):
+    step = len(eng) // (k * per)
+    eng = eng[::step][:k * per]
     return [_bits(eng[i::k]) for i in range(k)]
 
 
@@ -58,16 +66,19 @@ def _plan(T, topo):
                 h = [q for q in h if not all(topo.may_write(q, x) for x in cores)] or h
             relay.append((h[0], d))
             free.remove(h[0])
-        a = [p for p in relay if topo.die(p[0]) == topo.die(c)]
-        b = [p for p in relay if topo.die(p[0]) != topo.die(c)]
-        mixed = []
-        while a or b:
-            if a:
-                mixed.append(a.pop(0))
-            if b:
-                mixed.append(b.pop(0))
-        plan.append({"relay": mixed, "direct": near[extra:]})
+        plan.append({"relay": relay, "direct": near[extra:]})
     return plan
+
+
+def _order(plan, r):
+    early = [s for s, p in enumerate(plan) if r in p["direct"]]
+    late = [s for s, p in enumerate(plan) if r in [d for _, d in p["relay"]]]
+    return early, late
+
+
+def _slot(plan, r, s):
+    early, late = _order(plan, r)
+    return TK * (early + late).index(s)
 
 
 def _dst(topo, c):
@@ -75,13 +86,18 @@ def _dst(topo, c):
     return DstId(rid=rid, pnc=pid)
 
 
-def _helper(g, core, T, topo, s, d):
+def _blocks(ys, pair):
+    a, b = pair
+    return ys[:, a:b + 1:b - a, :]
+
+
+def _helper(g, core, T, topo, plan, s, d):
     to = T.cores[d]
-    eng = _engines(topo.mask(core, to))
-    step = len(eng) // N2
     rid, pid, _ = topo.addr(to)
+    mask = _deal(_common(topo, core, [to]), 1, N2)[0]
+    at = _slot(plan, d, s)
     g.wait_ge(T.sem.hop, N1)
-    g.remote_dma(T.land[:, TK * s:TK * s + TK], T.relay[:], T.sem.arrived, T.sem.sent, pid, rid, _bits(eng[::step]))
+    g.remote_dma(T.land[:, at:at + TK], T.relay[:], T.sem.arrl, T.sem.sent, pid, rid, mask)
     g.wait_ge(T.sem.sent, N2)
 
 
@@ -92,51 +108,57 @@ def rank_program(g, core, T, topo):
         for s, p in enumerate(plan):
             for h, d in p["relay"]:
                 if h == core:
-                    _helper(g, core, T, topo, s, d)
+                    _helper(g, core, T, topo, plan, s, d)
         return
 
     mine = plan[rank]
-    cols = NR * TK
     own = TK * rank
-
-    g.sync.dma_start(T.xs[:], T.x[:, :]).then_inc(T.sem.ldx, 16)
-    g.sync.dma_start(T.ws[:], T.w[:, :]).then_inc(T.sem.ldw, 16)
-
-    g.wait_ge(T.sem.ldx, 16)
+    peers = [T.cores[d] for d in mine["direct"]]
     helpers = [h for h, _ in mine["relay"]]
-    masks = _deal(core, helpers, N1, topo)
+
+    queues = [g.sync, g.scalar]
+    for k, (_, d) in enumerate(mine["relay"]):
+        queues[k % 2].dma_start(T.xb[k], T.x[:, TK * d:TK * d + TK]).then_inc(T.sem.ldb, 16)
+    g.sync.dma_start(T.xs[:], T.x[:, :]).then_inc(T.sem.ldx, 16)
+    g.scalar.dma_start(T.ws[:], T.w[:, :]).then_inc(T.sem.ldw, 16)
+
+    g.wait_ge(T.sem.ldb, 16 * len(helpers))
     g.remote_dma_fused(
         [RemoteDMATransfer(dst_ids=[_dst(topo, h)], dma_engine_mask=m, remote_sem=T.sem.hop,
-                           src=T.xs[:, TK * d:TK * d + TK], dst=T.relay[:])
-         for (h, d), m in zip(mine["relay"], masks)],
+                           src=T.xb[k], dst=T.relay[:])
+         for k, (h, m) in enumerate(zip(helpers, _deal(_common(topo, core, helpers), len(helpers), N1)))],
         local_sem=T.sem.sent)
-    peers = [T.cores[d] for d in mine["direct"]]
-    masks = _deal(core, peers, ND, topo)
+    g.wait_ge(T.sem.ldx, 16)
     g.remote_dma_fused(
-        [RemoteDMATransfer(dst_ids=[_dst(topo, T.cores[d])], dma_engine_mask=m, remote_sem=T.sem.arrived,
-                           src=T.xs[:, TK * d:TK * d + TK], dst=T.land[:, own:own + TK])
-         for d, m in zip(mine["direct"], masks)],
+        [RemoteDMATransfer(dst_ids=[_dst(topo, T.cores[d])], dma_engine_mask=m, remote_sem=T.sem.arre,
+                           src=T.xs[:, TK * d:TK * d + TK],
+                           dst=T.land[:, _slot(plan, d, rank):_slot(plan, d, rank) + TK])
+         for d, m in zip(mine["direct"], _deal(_common(topo, core, peers), len(peers), ND))],
         local_sem=T.sem.sent)
 
-    expect = 0
-    for s, p in enumerate(plan):
-        expect += N2 * len([1 for _, d in p["relay"] if d == rank]) + ND * len([1 for d in p["direct"] if d == rank])
+    early, late = _order(plan, rank)
+    two = 2 * TK
 
     g.tensor.wait_ge(T.sem.ldw, 16)
     g.tensor.wait_ge(T.sem.ldx, 16)
-    g.tensor.matmul(T.acc[:, own:own + TK], T.ws[:], T.xs[:, own:own + TK], start=True, stop=True).then_inc(T.sem.mm, 1)
-    g.tensor.wait_ge(T.sem.arrived, expect)
-    done = 1
-    for a, b in ((0, own), (own + TK, cols)):
-        if b > a:
-            g.tensor.matmul(T.acc[:, a:b], T.ws[:], T.land[:, a:b], start=True, stop=True).then_inc(T.sem.mm, 1)
-            done += 1
+    g.tensor.matmul(T.acco[:, 0:TK], T.ws[:], T.xs[:, own:own + TK], start=True, stop=True).then_inc(T.sem.mmo, 1)
+    g.tensor.wait_ge(T.sem.arre, ND * len(early))
+    g.tensor.matmul(T.acce[:, 0:two], T.ws[:], T.land[:, 0:two], start=True, stop=True).then_inc(T.sem.mme, 1)
+    g.tensor.wait_ge(T.sem.arrl, N2 * len(late))
+    g.tensor.matmul(T.acc1[:, 0:two], T.ws[:], T.land[:, two:2 * two], start=True, stop=True).then_inc(T.sem.mm1, 1)
+    g.tensor.matmul(T.acc2[:, 0:two], T.ws[:], T.land[:, 2 * two:3 * two], start=True, stop=True).then_inc(T.sem.mm2, 1)
 
-    g.vector.wait_ge(T.sem.mm, done)
-    g.vector.tensor_copy(T.ys[:], T.acc[:, 0:cols]).then_inc(T.sem.cp, 1)
+    g.vector.wait_ge(T.sem.mmo, 1)
+    g.vector.tensor_copy(T.ys[:, rank, :], T.acco[:, 0:TK]).then_inc(T.sem.cp, 1)
+    g.vector.wait_ge(T.sem.mme, 1)
+    g.vector.tensor_copy(_blocks(T.ys, early), T.acce[:, 0:two]).then_inc(T.sem.cp, 1)
+    g.vector.wait_ge(T.sem.mm1, 1)
+    g.vector.tensor_copy(_blocks(T.ys, late[0:2]), T.acc1[:, 0:two]).then_inc(T.sem.cp, 1)
+    g.vector.wait_ge(T.sem.mm2, 1)
+    g.vector.tensor_copy(_blocks(T.ys, late[2:4]), T.acc2[:, 0:two]).then_inc(T.sem.cp, 1)
 
-    g.sync.wait_ge(T.sem.cp, 1)
+    g.sync.wait_ge(T.sem.cp, 4)
     g.sync.dma_start(T.y[:, :], T.ys[:]).then_inc(T.sem.st, 16)
     g.sync.wait_ge(T.sem.st, 16)
 
-    g.wait_ge(T.sem.sent, N1 * len(mine["relay"]) + ND * len(mine["direct"]))
+    g.wait_ge(T.sem.sent, N1 * len(helpers) + ND * len(peers))

@@ -14,13 +14,15 @@ SCRATCH = {
     "ws": ("sbuf", [128, 128], "bfloat16"),
     "land": ("sbuf", [128, (NR - 1) * TK], "bfloat16"),
     "relay": ("dram", [128, TK], "bfloat16"),
+    "relay2": ("dram", [128, TK], "bfloat16"),
     "ys": ("sbuf", [128, NR, TK], "bfloat16"),
     "acco": ("psum", [128, 512], "float32"),
     "acce": ("psum", [128, 512], "float32"),
     "acc1": ("psum", [128, 512], "float32"),
     "acc2": ("psum", [128, 512], "float32"),
 }
-SEMAPHORES = ["ldb", "ldx", "ldw", "hop", "arre", "arrl", "sent", "mmo", "mme", "mm1", "mm2", "cp", "st"]
+SEMAPHORES = ["lda", "ldb", "ldd", "ldx", "ldw", "hop", "hop2", "arre", "arr1", "arr2", "sent",
+              "mmo", "mme", "mm1", "mm2", "cp", "st"]
 
 
 def _engines(mask):
@@ -57,28 +59,28 @@ def _plan(T, topo):
         far = [d for d in peers if not topo.may_write(c, cores[d])]
         near = [d for d in peers if topo.may_write(c, cores[d])]
         extra = max(0, len(near) - DIRECT)
-        free = [h for h in everyone if topo.chip(h) == topo.chip(c) and h not in cores]
+        long_way = [d for d in far if not topo.mates(topo.chip(c), topo.chip(cores[d]))]
+        order = long_way + [d for d in far if d not in long_way] + near[:extra]
+        when = {}
+        for k, d in enumerate(order):
+            when[d] = 0 if k == 0 else 1 if k == RELAYED - 1 else 3 if d in long_way else 2
+        free = [h for h in everyone if topo.chip(h) == topo.chip(c) and h not in cores
+                and all(topo.may_write(h, x) for x in cores)]
         free.sort(key=lambda h: (topo.die(h) != topo.die(c), h))
-        relay = []
-        for d in far + near[:extra]:
-            h = [h for h in free if topo.may_write(h, cores[d])]
-            if d not in far:
-                h = [q for q in h if not all(topo.may_write(q, x) for x in cores)] or h
-            relay.append((h[0], d))
-            free.remove(h[0])
-        plan.append({"relay": relay, "direct": near[extra:]})
+        plan.append({"order": order, "when": when, "helpers": free[:RELAYED - 1], "direct": near[extra:]})
     return plan
 
 
 def _order(plan, r):
     early = [s for s, p in enumerate(plan) if r in p["direct"]]
-    late = [s for s, p in enumerate(plan) if r in [d for _, d in p["relay"]]]
-    return early, late
+    late = sorted((p["when"][r], s) for s, p in enumerate(plan) if r in p["order"])
+    late = [s for _, s in late]
+    return early, sorted(late[0:2]), sorted(late[2:4])
 
 
 def _slot(plan, r, s):
-    early, late = _order(plan, r)
-    return TK * (early + late).index(s)
+    e, a, b = _order(plan, r)
+    return TK * (e + a + b).index(s)
 
 
 def _dst(topo, c):
@@ -91,14 +93,14 @@ def _blocks(ys, pair):
     return ys[:, a:b + 1:b - a, :]
 
 
-def _helper(g, core, T, topo, plan, s, d):
+def _pass_on(g, core, T, topo, plan, s, d, buf, hop):
     to = T.cores[d]
     rid, pid, _ = topo.addr(to)
     mask = _deal(_common(topo, core, [to]), 1, N2)[0]
     at = _slot(plan, d, s)
-    g.wait_ge(T.sem.hop, N1)
-    g.remote_dma(T.land[:, at:at + TK], T.relay[:], T.sem.arrl, T.sem.sent, pid, rid, mask)
-    g.wait_ge(T.sem.sent, N2)
+    arr = T.sem.arr1 if s in _order(plan, d)[1] else T.sem.arr2
+    g.wait_ge(hop, N1)
+    g.remote_dma(T.land[:, at:at + TK], buf[:], arr, T.sem.sent, pid, rid, mask)
 
 
 def rank_program(g, core, T, topo):
@@ -106,28 +108,45 @@ def rank_program(g, core, T, topo):
     rank = T.rank_of(core)
     if rank is None:
         for s, p in enumerate(plan):
-            for h, d in p["relay"]:
-                if h == core:
-                    _helper(g, core, T, topo, plan, s, d)
+            if core in p["helpers"]:
+                k = p["helpers"].index(core)
+                _pass_on(g, core, T, topo, plan, s, p["order"][k], T.relay, T.sem.hop)
+                if k == 0:
+                    _pass_on(g, core, T, topo, plan, s, p["order"][RELAYED - 1], T.relay2, T.sem.hop2)
+                g.wait_ge(T.sem.sent, N2 * (2 if k == 0 else 1))
         return
 
     mine = plan[rank]
     own = TK * rank
+    order = mine["order"]
+    helpers = mine["helpers"]
     peers = [T.cores[d] for d in mine["direct"]]
-    helpers = [h for h, _ in mine["relay"]]
 
-    queues = [g.sync, g.scalar]
-    for k, (_, d) in enumerate(mine["relay"]):
-        queues[k % 2].dma_start(T.xb[k], T.x[:, TK * d:TK * d + TK]).then_inc(T.sem.ldb, 16)
-    g.sync.dma_start(T.xs[:], T.x[:, :]).then_inc(T.sem.ldx, 16)
-    g.scalar.dma_start(T.ws[:], T.w[:, :]).then_inc(T.sem.ldw, 16)
+    def cut(q, k, sem):
+        d = order[k]
+        q.dma_start(T.xb[k], T.x[:, TK * d:TK * d + TK]).then_inc(sem, 16)
 
-    g.wait_ge(T.sem.ldb, 16 * len(helpers))
-    g.remote_dma_fused(
-        [RemoteDMATransfer(dst_ids=[_dst(topo, h)], dma_engine_mask=m, remote_sem=T.sem.hop,
-                           src=T.xb[k], dst=T.relay[:])
-         for k, (h, m) in enumerate(zip(helpers, _deal(_common(topo, core, helpers), len(helpers), N1)))],
-        local_sem=T.sem.sent)
+    d0 = order[0]
+    g.sync.dma_start(T.xb[0, 0:64, :], T.x[0:64, TK * d0:TK * d0 + TK]).then_inc(T.sem.lda, 16)
+    g.scalar.dma_start(T.xb[0, 64:128, :], T.x[64:128, TK * d0:TK * d0 + TK]).then_inc(T.sem.lda, 16)
+    cut(g.sync, 1, T.sem.ldb)
+    cut(g.scalar, 2, T.sem.ldb)
+    cut(g.sync, 3, T.sem.ldd)
+    g.scalar.dma_start(T.xs[:], T.x[:, :]).then_inc(T.sem.ldx, 16)
+    g.sync.dma_start(T.ws[:], T.w[:, :]).then_inc(T.sem.ldw, 16)
+
+    ma, mb = _deal(_common(topo, core, helpers), 2, N1)
+
+    def hand(k, h, m, buf, sem):
+        return RemoteDMATransfer(dst_ids=[_dst(topo, h)], dma_engine_mask=m, remote_sem=sem, src=T.xb[k], dst=buf[:])
+
+    g.wait_ge(T.sem.lda, 32)
+    g.remote_dma_fused([hand(0, helpers[0], ma, T.relay, T.sem.hop)], local_sem=T.sem.sent)
+    g.wait_ge(T.sem.ldb, 32)
+    g.remote_dma_fused([hand(1, helpers[1], mb, T.relay, T.sem.hop), hand(2, helpers[2], ma, T.relay, T.sem.hop)],
+                       local_sem=T.sem.sent)
+    g.wait_ge(T.sem.ldd, 16)
+    g.remote_dma_fused([hand(3, helpers[0], mb, T.relay2, T.sem.hop2)], local_sem=T.sem.sent)
     g.wait_ge(T.sem.ldx, 16)
     g.remote_dma_fused(
         [RemoteDMATransfer(dst_ids=[_dst(topo, T.cores[d])], dma_engine_mask=m, remote_sem=T.sem.arre,
@@ -136,7 +155,7 @@ def rank_program(g, core, T, topo):
          for d, m in zip(mine["direct"], _deal(_common(topo, core, peers), len(peers), ND))],
         local_sem=T.sem.sent)
 
-    early, late = _order(plan, rank)
+    early, first, last = _order(plan, rank)
     two = 2 * TK
 
     g.tensor.wait_ge(T.sem.ldw, 16)
@@ -144,8 +163,9 @@ def rank_program(g, core, T, topo):
     g.tensor.matmul(T.acco[:, 0:TK], T.ws[:], T.xs[:, own:own + TK], start=True, stop=True).then_inc(T.sem.mmo, 1)
     g.tensor.wait_ge(T.sem.arre, ND * len(early))
     g.tensor.matmul(T.acce[:, 0:two], T.ws[:], T.land[:, 0:two], start=True, stop=True).then_inc(T.sem.mme, 1)
-    g.tensor.wait_ge(T.sem.arrl, N2 * len(late))
+    g.tensor.wait_ge(T.sem.arr1, N2 * len(first))
     g.tensor.matmul(T.acc1[:, 0:two], T.ws[:], T.land[:, two:2 * two], start=True, stop=True).then_inc(T.sem.mm1, 1)
+    g.tensor.wait_ge(T.sem.arr2, N2 * len(last))
     g.tensor.matmul(T.acc2[:, 0:two], T.ws[:], T.land[:, 2 * two:3 * two], start=True, stop=True).then_inc(T.sem.mm2, 1)
 
     g.vector.wait_ge(T.sem.mmo, 1)
@@ -153,12 +173,12 @@ def rank_program(g, core, T, topo):
     g.vector.wait_ge(T.sem.mme, 1)
     g.vector.tensor_copy(_blocks(T.ys, early), T.acce[:, 0:two]).then_inc(T.sem.cp, 1)
     g.vector.wait_ge(T.sem.mm1, 1)
-    g.vector.tensor_copy(_blocks(T.ys, late[0:2]), T.acc1[:, 0:two]).then_inc(T.sem.cp, 1)
+    g.vector.tensor_copy(_blocks(T.ys, first), T.acc1[:, 0:two]).then_inc(T.sem.cp, 1)
     g.vector.wait_ge(T.sem.mm2, 1)
-    g.vector.tensor_copy(_blocks(T.ys, late[2:4]), T.acc2[:, 0:two]).then_inc(T.sem.cp, 1)
+    g.vector.tensor_copy(_blocks(T.ys, last), T.acc2[:, 0:two]).then_inc(T.sem.cp, 1)
 
     g.sync.wait_ge(T.sem.cp, 4)
     g.sync.dma_start(T.y[:, :], T.ys[:]).then_inc(T.sem.st, 16)
     g.sync.wait_ge(T.sem.st, 16)
 
-    g.wait_ge(T.sem.sent, N1 * len(helpers) + ND * len(peers))
+    g.wait_ge(T.sem.sent, N1 * RELAYED + ND * len(peers))

from concourse.bass import DstId, RemoteDMATransfer

TK = 32
NR = 7
DIRECT = 2
RELAYED = NR - 1 - DIRECT
N1 = 2
N2 = 8
ND = 4

SCRATCH = {
    "xb": ("dram", [RELAYED, 128, TK], "bfloat16"),
    "xs": ("sbuf", [128, NR * TK], "bfloat16"),
    "ws": ("sbuf", [128, 128], "bfloat16"),
    "land": ("sbuf", [128, (NR - 1) * TK], "bfloat16"),
    "relay": ("dram", [128, TK], "bfloat16"),
    "relay2": ("dram", [128, TK], "bfloat16"),
    "ys": ("sbuf", [128, NR, TK], "bfloat16"),
    "acco": ("psum", [128, 512], "float32"),
    "acce": ("psum", [128, 512], "float32"),
    "acc1": ("psum", [128, 512], "float32"),
    "acc2": ("psum", [128, 512], "float32"),
}
SEMAPHORES = ["lda", "ldb", "ldd", "ldx", "ldw", "hop", "hop2", "arre", "arr1", "arr2", "sent",
              "mmo", "mme", "mm1", "mm2", "cp", "st"]


def _engines(mask):
    return [e for e in range(mask.bit_length()) if (mask >> e) & 1]


def _bits(engines):
    m = 0
    for e in engines:
        m |= 1 << e
    return m


def _common(topo, src, dsts):
    m = topo.mask(src, dsts[0])
    for d in dsts:
        m &= topo.mask(src, d)
    return _engines(m)


def _deal(eng, k, per):
    step = len(eng) // (k * per)
    eng = eng[::step][:k * per]
    return [_bits(eng[i::k]) for i in range(k)]


def _plan(T, topo):
    cores = list(T.cores)
    n = len(cores)
    everyone = range(topo.CHIPS * topo.CORES_PER_CHIP)
    plan = []
    for s, c in enumerate(cores):
        peers = [(s + k) % n for k in range(1, n)]
        far = [d for d in peers if not topo.may_write(c, cores[d])]
        near = [d for d in peers if topo.may_write(c, cores[d])]
        extra = max(0, len(near) - DIRECT)
        long_way = [d for d in far if not topo.mates(topo.chip(c), topo.chip(cores[d]))]
        order = long_way + [d for d in far if d not in long_way] + near[:extra]
        when = {}
        for k, d in enumerate(order):
            when[d] = 0 if k == 0 else 1 if k == RELAYED - 1 else 3 if d in long_way else 2
        free = [h for h in everyone if topo.chip(h) == topo.chip(c) and h not in cores
                and all(topo.may_write(h, x) for x in cores)]
        free.sort(key=lambda h: (topo.die(h) != topo.die(c), h))
        plan.append({"order": order, "when": when, "helpers": free[:RELAYED - 1], "direct": near[extra:]})
    return plan


def _order(plan, r):
    early = [s for s, p in enumerate(plan) if r in p["direct"]]
    late = sorted((p["when"][r], s) for s, p in enumerate(plan) if r in p["order"])
    late = [s for _, s in late]
    return early, sorted(late[0:2]), sorted(late[2:4])


def _slot(plan, r, s):
    e, a, b = _order(plan, r)
    return TK * (e + a + b).index(s)


def _dst(topo, c):
    rid, pid, _ = topo.addr(c)
    return DstId(rid=rid, pnc=pid)


def _blocks(ys, pair):
    a, b = pair
    return ys[:, a:b + 1:b - a, :]


def _pass_on(g, core, T, topo, plan, s, d, buf, hop):
    to = T.cores[d]
    rid, pid, _ = topo.addr(to)
    mask = _deal(_common(topo, core, [to]), 1, N2)[0]
    at = _slot(plan, d, s)
    arr = T.sem.arr1 if s in _order(plan, d)[1] else T.sem.arr2
    g.wait_ge(hop, N1)
    g.remote_dma(T.land[:, at:at + TK], buf[:], arr, T.sem.sent, pid, rid, mask)


def rank_program(g, core, T, topo):
    plan = _plan(T, topo)
    rank = T.rank_of(core)
    if rank is None:
        for s, p in enumerate(plan):
            if core in p["helpers"]:
                k = p["helpers"].index(core)
                _pass_on(g, core, T, topo, plan, s, p["order"][k], T.relay, T.sem.hop)
                if k == 0:
                    _pass_on(g, core, T, topo, plan, s, p["order"][RELAYED - 1], T.relay2, T.sem.hop2)
                g.wait_ge(T.sem.sent, N2 * (2 if k == 0 else 1))
        return

    mine = plan[rank]
    own = TK * rank
    order = mine["order"]
    helpers = mine["helpers"]
    peers = [T.cores[d] for d in mine["direct"]]

    def cut(q, k, sem):
        d = order[k]
        q.dma_start(T.xb[k], T.x[:, TK * d:TK * d + TK]).then_inc(sem, 16)

    d0 = order[0]
    g.sync.dma_start(T.xb[0, 0:64, :], T.x[0:64, TK * d0:TK * d0 + TK]).then_inc(T.sem.lda, 16)
    g.scalar.dma_start(T.xb[0, 64:128, :], T.x[64:128, TK * d0:TK * d0 + TK]).then_inc(T.sem.lda, 16)
    cut(g.sync, 1, T.sem.ldb)
    cut(g.scalar, 2, T.sem.ldb)
    cut(g.sync, 3, T.sem.ldd)
    g.scalar.dma_start(T.xs[:], T.x[:, :]).then_inc(T.sem.ldx, 16)
    g.sync.dma_start(T.ws[:], T.w[:, :]).then_inc(T.sem.ldw, 16)

    ma, mb = _deal(_common(topo, core, helpers), 2, N1)

    def hand(k, h, m, buf, sem):
        return RemoteDMATransfer(dst_ids=[_dst(topo, h)], dma_engine_mask=m, remote_sem=sem, src=T.xb[k], dst=buf[:])

    g.wait_ge(T.sem.lda, 32)
    g.remote_dma_fused([hand(0, helpers[0], ma, T.relay, T.sem.hop)], local_sem=T.sem.sent)
    g.wait_ge(T.sem.ldb, 32)
    g.remote_dma_fused([hand(1, helpers[1], mb, T.relay, T.sem.hop), hand(2, helpers[2], ma, T.relay, T.sem.hop)],
                       local_sem=T.sem.sent)
    g.wait_ge(T.sem.ldd, 16)
    g.remote_dma_fused([hand(3, helpers[0], mb, T.relay2, T.sem.hop2)], local_sem=T.sem.sent)
    g.wait_ge(T.sem.ldx, 16)
    g.remote_dma_fused(
        [RemoteDMATransfer(dst_ids=[_dst(topo, T.cores[d])], dma_engine_mask=m, remote_sem=T.sem.arre,
                           src=T.xs[:, TK * d:TK * d + TK],
                           dst=T.land[:, _slot(plan, d, rank):_slot(plan, d, rank) + TK])
         for d, m in zip(mine["direct"], _deal(_common(topo, core, peers), len(peers), ND))],
        local_sem=T.sem.sent)

    early, first, last = _order(plan, rank)
    two = 2 * TK

    g.tensor.wait_ge(T.sem.ldw, 16)
    g.tensor.wait_ge(T.sem.ldx, 16)
    g.tensor.matmul(T.acco[:, 0:TK], T.ws[:], T.xs[:, own:own + TK], start=True, stop=True).then_inc(T.sem.mmo, 1)
    g.tensor.wait_ge(T.sem.arre, ND * len(early))
    g.tensor.matmul(T.acce[:, 0:two], T.ws[:], T.land[:, 0:two], start=True, stop=True).then_inc(T.sem.mme, 1)
    g.tensor.wait_ge(T.sem.arr1, N2 * len(first))
    g.tensor.matmul(T.acc1[:, 0:two], T.ws[:], T.land[:, two:2 * two], start=True, stop=True).then_inc(T.sem.mm1, 1)
    g.tensor.wait_ge(T.sem.arr2, N2 * len(last))
    g.tensor.matmul(T.acc2[:, 0:two], T.ws[:], T.land[:, 2 * two:3 * two], start=True, stop=True).then_inc(T.sem.mm2, 1)

    g.vector.wait_ge(T.sem.mmo, 1)
    g.vector.tensor_copy(T.ys[:, rank, :], T.acco[:, 0:TK]).then_inc(T.sem.cp, 1)
    g.vector.wait_ge(T.sem.mme, 1)
    g.vector.tensor_copy(_blocks(T.ys, early), T.acce[:, 0:two]).then_inc(T.sem.cp, 1)
    g.vector.wait_ge(T.sem.mm1, 1)
    g.vector.tensor_copy(_blocks(T.ys, first), T.acc1[:, 0:two]).then_inc(T.sem.cp, 1)
    g.vector.wait_ge(T.sem.mm2, 1)
    g.vector.tensor_copy(_blocks(T.ys, last), T.acc2[:, 0:two]).then_inc(T.sem.cp, 1)

    g.sync.wait_ge(T.sem.cp, 4)
    g.sync.dma_start(T.y[:, :], T.ys[:]).then_inc(T.sem.st, 16)
    g.sync.wait_ge(T.sem.st, 16)

    g.wait_ge(T.sem.sent, N1 * RELAYED + ND * len(peers))
